import numpy as np
import ml_dtypes


def mxq(x, axis, fmt="e4m3"):
    dtype, down = {"e4m3": (ml_dtypes.float8_e4m3fn, 7), "e5m2": (ml_dtypes.float8_e5m2, 14)}[fmt]
    v = np.moveaxis(np.asarray(x, np.float32).astype(ml_dtypes.bfloat16).astype(np.float64), axis, -1)
    blocks = v.reshape(v.shape[:-1] + (-1, 32))
    amax = np.abs(blocks).max(-1, keepdims=True)
    byte = np.maximum(np.where(amax > 0, np.frexp(amax)[1] - 1 + 127, 0) - down, 1)
    scale = np.exp2(byte - 127.0)
    codes = (blocks / scale).astype(np.float32).astype(dtype).astype(np.float64)
    return np.moveaxis((codes * scale).reshape(v.shape), -1, axis)


WIDE = False


def mx_kscale(k):
    if not WIDE:
        return np.ones(k)
    levels = np.array([30, -30])
    if k % 512:
        return np.exp2(np.random.permutation(np.resize(levels, k // 32))).repeat(32)
    a = np.empty((k // 512, 16))
    for p in range(k // 512):
        a[p, :8] = np.random.permutation(np.resize(levels, 8))
        for g in range(8):
            far = levels[np.abs(levels - a[p, g]) >= 10]
            a[p, g + 8] = far[np.random.randint(len(far))]
    return np.exp2(a.ravel()).repeat(32)


def f64(x):
    return np.asarray(x).astype(np.float64)


T, D, H = 1024, 1280, 2048


def setup_inputs():
    n = np.random.standard_normal
    s1 = mx_kscale(T)[:, None]
    s2 = mx_kscale(T)[:, None]
    m = np.exp(0.5 * n((T, 1)))
    return {
        "x": (n((T, D)) * s1).astype(np.float32),
        "de": (m * n((T, H)) / np.sqrt(T) / s1).astype(np.float32),
        "dr": (m * n((T, D)) / np.sqrt(T) * s2).astype(np.float32),
        "e": (n((T, H)) / s2).astype(np.float32),
    }


def reference(x, de, dr, e):
    x_ = mxq(f64(x), 0, "e4m3")
    de_ = mxq(f64(de), 0, "e5m2")
    dr_ = mxq(f64(dr), 0, "e5m2")
    e_ = mxq(f64(e), 0, "e4m3")
    y = x_.T @ de_ + dr_.T @ e_
    return y

@@ -1,0 +1,172 @@
+from contextlib import ExitStack
+
+import concourse.mybir as mybir
+
+T, D, H = 1024, 1280, 2048
+FLOPS = 2 * (2 * T * D * H)
+
+F32 = mybir.dt.float32
+BF16 = mybir.dt.bfloat16
+U32 = mybir.dt.uint32
+U8 = mybir.dt.uint8
+E4M3 = mybir.dt.float8_e4m3fn_x4
+E5M2 = mybir.dt.float8_e5m2_x4
+
+P = 128
+PACK = 4
+T_PASS = P * PACK
+D_TILE = 128
+H_TILE = 512
+HALF = H // 2
+D_TILES = D // D_TILE
+
+RAW_BUFS = 4
+LOADS_AHEAD = RAW_BUFS - 1
+OPEN_TILES = 8
+
+
+def tile_mix_tied_none_kernel(tc, x, de, dr, e, out):
+    nc = tc.nc
+    with ExitStack() as ctx:
+        keep = ctx.enter_context(tc.tile_pool(name="keep", bufs=1))
+        raws = ctx.enter_context(tc.tile_pool(name="raws", bufs=RAW_BUFS))
+        mids = ctx.enter_context(tc.tile_pool(name="mids", bufs=3))
+        outs = ctx.enter_context(tc.tile_pool(name="outs", bufs=14))
+        psum = ctx.enter_context(tc.psum_pool(name="psum", bufs=OPEN_TILES))
+        ctx.enter_context(tc.manual_schedule())
+
+        codes, scales = {}, {}
+        sources = {"x": (x, E4M3), "de": (de, E5M2), "dr": (dr, E5M2), "e": (e, E4M3)}
+        for op in sources:
+            width = sources[op][0].shape[1]
+            for c in range(T // T_PASS):
+                codes[op, c] = keep.tile([P, width], U32, name=f"codes_{op}{c}", align_bytes=64)
+                scales[op, c] = keep.tile([P, width], U8, name=f"scales_{op}{c}", align_bytes=64)
+
+        wide = (("v", 512), ("s", 512), ("v", 256))
+        pair = (("v", 512), ("s", 512))
+        fine = (("v", 256), ("s", 256))
+        loads = [("x", 0, 0, wide), ("x", 1, 0, wide), ("dr", 0, 0, wide), ("dr", 1, 0, wide)]
+        loads += [("de", 0, 0, pair), ("de", 1, 0, pair), ("e", 0, 0, pair), ("e", 1, 0, fine), ("e", 1, H_TILE, fine)]
+        loads += [("de", 0, HALF, pair), ("de", 1, HALF, pair), ("e", 0, HALF, pair), ("e", 1, HALF, pair)]
+        staged = {}
+
+        def load(i):
+            if i >= len(loads):
+                return
+            op, c, col, pieces = loads[i]
+            width = sum(p[1] for p in pieces)
+            raw = raws.tile([P, PACK * D], F32, name="raw", align_bytes=64)
+            view = raw[:, 0 : PACK * width].rearrange("p (j w) -> p j w", j=PACK)
+            rows = sources[op][0][c * T_PASS : (c + 1) * T_PASS, col : col + width]
+            nc.sync.dma_start(out=view, in_=rows.rearrange("(p j) w -> p j w", j=PACK))
+            staged[i] = view
+
+        def quantize(i):
+            op, c, col, pieces = loads[i]
+            view = staged[i]
+            mid = {}
+            at = 0
+            for n, (eng, w) in enumerate(pieces):
+                m = mids.tile([P, H_TILE * PACK], BF16, name="mid_" + eng, align_bytes=64)
+                dst = m[:, 0 : w * PACK].rearrange("p (g i j) -> p g j i", i=4, j=PACK)
+                src = view[:, :, at : at + w].rearrange("p j (g i) -> p g j i", i=4)
+                if eng == "v":
+                    nc.vector.tensor_copy(out=dst, in_=src)
+                else:
+                    nc.scalar.copy(out=dst, in_=src)
+                mid[n] = (m, at, w)
+                at += w
+            order = [n for n in range(len(pieces)) if pieces[n][0] == "v"] + [n for n in range(len(pieces)) if pieces[n][0] == "s"]
+            for n in order:
+                m, at, w = mid[n]
+                cols = slice(col + at, col + at + w)
+                nc.vector.quantize_mx(
+                    out=codes[op, c][:, cols].bitcast(sources[op][1]),
+                    scales=scales[op, c][:, cols],
+                    in_=m[:, 0 : w * PACK],
+                )
+
+        def step(i):
+            load(i + LOADS_AHEAD)
+            quantize(i)
+
+        passes = (("x", "de", 0), ("x", "de", 1), ("dr", "e", 0), ("dr", "e", 1))
+        acc, result = {}, {}
+        count = [0]
+
+        def multiply(d, q, k):
+            left, right, c = passes[k]
+            if k == 0:
+                acc[d, q] = psum.tile([P, H_TILE], F32, name="acc")
+            dc = slice(d * D_TILE, (d + 1) * D_TILE)
+            hc = slice(q * H_TILE, (q + 1) * H_TILE)
+            nc.tensor.matmul_mx(
+                out=acc[d, q][:],
+                lhsT=codes[left, c][:, dc].bitcast(sources[left][1]),
+                lhsT_scale=scales[left, c][:, dc],
+                rhs=codes[right, c][:, hc].bitcast(sources[right][1]),
+                rhs_scale=scales[right, c][:, hc],
+                start=(k == 0),
+                stop=(k == len(passes) - 1),
+            )
+
+        def finish(d, q):
+            half, odd = q // 2, q % 2
+            if odd == 0:
+                result[d, half] = outs.tile([P, HALF], F32, name="result", align_bytes=64)
+            r = result[d, half]
+            cols = slice(odd * H_TILE, (odd + 1) * H_TILE)
+            if count[0] % 2 == 0:
+                nc.vector.tensor_copy(out=r[:, cols], in_=acc[d, q][:])
+            else:
+                nc.scalar.copy(out=r[:, cols], in_=acc[d, q][:])
+            count[0] += 1
+            dr_ = slice(d * D_TILE, (d + 1) * D_TILE)
+            if (d, half) == (D_TILES - 1, 1):
+                nc.sync.dma_start(out=out[dr_, q * H_TILE : (q + 1) * H_TILE], in_=r[:, cols])
+            elif odd == 1:
+                nc.sync.dma_start(out=out[dr_, half * HALF : (half + 1) * HALF], in_=r[:])
+
+        def whole(d, q):
+            for k in range(4):
+                multiply(d, q, k)
+            finish(d, q)
+
+        for i in range(LOADS_AHEAD):
+            load(i)
+        for i in range(4):
+            step(i)
+        first = [(d, 0) for d in range(OPEN_TILES)]
+        for k in range(4):
+            step(4 + k)
+            for d, q in first:
+                multiply(d, q, k)
+        for d, q in first[:2]:
+            finish(d, q)
+        step(8)
+        for d, q in first[2:]:
+            finish(d, q)
+        whole(8, 0)
+        whole(9, 0)
+        step(9)
+        for d in range(0, 4):
+            whole(d, 1)
+        step(10)
+        for d in range(4, 8):
+            whole(d, 1)
+        step(11)
+        for d in range(8, 10):
+            whole(d, 1)
+        second = [(d, q) for d in range(4) for q in (2, 3)]
+        for k in range(3):
+            for d, q in second:
+                multiply(d, q, k)
+        step(12)
+        for d, q in second:
+            multiply(d, q, 3)
+        for d, q in second:
+            finish(d, q)
+        for d in range(4, 10):
+            for q in (2, 3):
+                whole(d, q)

@@ -20,19 +20,17 @@ H_TILE = 512
 HALF = H // 2
 D_TILES = D // D_TILE
 
-RAW_BUFS = 4
-LOADS_AHEAD = RAW_BUFS - 1
-OPEN_TILES = 8
+
+EARLY = 4
 
 
 def tile_mix_tied_none_kernel(tc, x, de, dr, e, out):
     nc = tc.nc
     with ExitStack() as ctx:
         keep = ctx.enter_context(tc.tile_pool(name="keep", bufs=1))
-        raws = ctx.enter_context(tc.tile_pool(name="raws", bufs=RAW_BUFS))
-        mids = ctx.enter_context(tc.tile_pool(name="mids", bufs=3))
-        outs = ctx.enter_context(tc.tile_pool(name="outs", bufs=14))
-        psum = ctx.enter_context(tc.psum_pool(name="psum", bufs=OPEN_TILES))
+        narrow = ctx.enter_context(tc.tile_pool(name="narrow", bufs=5))
+        mids = ctx.enter_context(tc.tile_pool(name="mids", bufs=2))
+        psum = ctx.enter_context(tc.psum_pool(name="psum", bufs=8))
         ctx.enter_context(tc.manual_schedule())
 
         codes, scales = {}, {}
@@ -43,57 +41,47 @@ def tile_mix_tied_none_kernel(tc, x, de, dr, e, out):
                 codes[op, c] = keep.tile([P, width], U32, name=f"codes_{op}{c}", align_bytes=64)
                 scales[op, c] = keep.tile([P, width], U8, name=f"scales_{op}{c}", align_bytes=64)
 
-        wide = (("v", 512), ("s", 512), ("v", 256))
-        pair = (("v", 512), ("s", 512))
-        fine = (("v", 256), ("s", 256))
-        loads = [("x", 0, 0, wide), ("x", 1, 0, wide), ("dr", 0, 0, wide), ("dr", 1, 0, wide)]
-        loads += [("de", 0, 0, pair), ("de", 1, 0, pair), ("e", 0, 0, pair), ("e", 1, 0, fine), ("e", 1, H_TILE, fine)]
-        loads += [("de", 0, HALF, pair), ("de", 1, HALF, pair), ("e", 0, HALF, pair), ("e", 1, HALF, pair)]
+        passes = (("x", "de", 0), ("x", "de", 1), ("dr", "e", 0), ("dr", "e", 1))
+        loads = [(left, c, 0, D) for left, rr, c in passes]
+        loads += [(right, c, q * H_TILE, H_TILE) for q in range(4) for ll, right, c in passes]
         staged = {}
 
-        def load(i):
+        def load(i, pool):
             if i >= len(loads):
                 return
-            op, c, col, pieces = loads[i]
-            width = sum(p[1] for p in pieces)
-            raw = raws.tile([P, PACK * D], F32, name="raw", align_bytes=64)
-            view = raw[:, 0 : PACK * width].rearrange("p (j w) -> p j w", j=PACK)
+            op, c, col, width = loads[i]
+            raw = pool.tile([P, PACK, width], F32, name="raw", align_bytes=64)
             rows = sources[op][0][c * T_PASS : (c + 1) * T_PASS, col : col + width]
-            nc.sync.dma_start(out=view, in_=rows.rearrange("(p j) w -> p j w", j=PACK))
-            staged[i] = view
+            nc.sync.dma_start(out=raw[:], in_=rows.rearrange("(p j) w -> p j w", j=PACK))
+            staged[i] = raw
 
         def quantize(i):
-            op, c, col, pieces = loads[i]
-            view = staged[i]
-            mid = {}
-            at = 0
-            for n, (eng, w) in enumerate(pieces):
+            op, c, col, width = loads[i]
+            raw = staged[i]
+            pieces = [("v", 0, 512), ("s", 512, 512), ("v", 1024, 256)] if width == D else [("v", 0, 256), ("s", 256, 256)]
+            ready = []
+            for eng, at, w in pieces:
                 m = mids.tile([P, H_TILE * PACK], BF16, name="mid_" + eng, align_bytes=64)
                 dst = m[:, 0 : w * PACK].rearrange("p (g i j) -> p g j i", i=4, j=PACK)
-                src = view[:, :, at : at + w].rearrange("p j (g i) -> p g j i", i=4)
+                src = raw[:, :, at : at + w].rearrange("p j (g i) -> p g j i", i=4)
                 if eng == "v":
                     nc.vector.tensor_copy(out=dst, in_=src)
                 else:
                     nc.scalar.copy(out=dst, in_=src)
-                mid[n] = (m, at, w)
-                at += w
-            order = [n for n in range(len(pieces)) if pieces[n][0] == "v"] + [n for n in range(len(pieces)) if pieces[n][0] == "s"]
-            for n in order:
-                m, at, w = mid[n]
-                cols = slice(col + at, col + at + w)
-                nc.vector.quantize_mx(
-                    out=codes[op, c][:, cols].bitcast(sources[op][1]),
-                    scales=scales[op, c][:, cols],
-                    in_=m[:, 0 : w * PACK],
-                )
+                ready.append((eng, m, at, w))
+            for want in ("v", "s"):
+                for eng, m, at, w in ready:
+                    if eng == want:
+                        cols = slice(col + at, col + at + w)
+                        nc.vector.quantize_mx(
+                            out=codes[op, c][:, cols].bitcast(sources[op][1]),
+                            scales=scales[op, c][:, cols],
+                            in_=m[:, 0 : w * PACK],
+                        )
 
-        def step(i):
-            load(i + LOADS_AHEAD)
-            quantize(i)
-
-        passes = (("x", "de", 0), ("x", "de", 1), ("dr", "e", 0), ("dr", "e", 1))
         acc, result = {}, {}
         count = [0]
+        waiting = []
 
         def multiply(d, q, k):
             left, right, c = passes[k]
@@ -108,65 +96,72 @@ def tile_mix_tied_none_kernel(tc, x, de, dr, e, out):
                 rhs=codes[right, c][:, hc].bitcast(sources[right][1]),
                 rhs_scale=scales[right, c][:, hc],
                 start=(k == 0),
-                stop=(k == len(passes) - 1),
+                stop=(k == 3),
             )
 
+        def store(d, lo, hi):
+            nc.sync.dma_start(out=out[d * D_TILE : (d + 1) * D_TILE, lo:hi], in_=result[d][:, lo:hi])
+
         def finish(d, q):
-            half, odd = q // 2, q % 2
-            if odd == 0:
-                result[d, half] = outs.tile([P, HALF], F32, name="result", align_bytes=64)
-            r = result[d, half]
-            cols = slice(odd * H_TILE, (odd + 1) * H_TILE)
+            if q == 0:
+                result[d] = outs.tile([P, H], F32, name="result", align_bytes=64)
+            cols = slice(q * H_TILE, (q + 1) * H_TILE)
             if count[0] % 2 == 0:
-                nc.vector.tensor_copy(out=r[:, cols], in_=acc[d, q][:])
+                nc.vector.tensor_copy(out=result[d][:, cols], in_=acc[d, q][:])
             else:
-                nc.scalar.copy(out=r[:, cols], in_=acc[d, q][:])
+                nc.scalar.copy(out=result[d][:, cols], in_=acc[d, q][:])
             count[0] += 1
-            dr_ = slice(d * D_TILE, (d + 1) * D_TILE)
-            if (d, half) == (D_TILES - 1, 1):
-                nc.sync.dma_start(out=out[dr_, q * H_TILE : (q + 1) * H_TILE], in_=r[:, cols])
-            elif odd == 1:
-                nc.sync.dma_start(out=out[dr_, half * HALF : (half + 1) * HALF], in_=r[:])
+            if q == 1:
+                waiting.append((d, 0, HALF))
+            elif q == 2 and d < EARLY:
+                waiting.append((d, HALF, HALF + H_TILE))
+            elif q == 3:
+                waiting.append((d, HALF + (H_TILE if d < EARLY else 0), H))
+            if len(staged) == len(loads):
+                flush()
 
-        def whole(d, q):
+        def flush():
+            for d, lo, hi in waiting:
+                store(d, lo, hi)
+            waiting.clear()
+
+        with tc.tile_pool(name="whole", bufs=4) as whole:
+            for i in range(4):
+                load(i, whole)
+            for i in range(4):
+                load(i + 4, narrow)
+                quantize(i)
+
+        outs = ctx.enter_context(tc.tile_pool(name="outs", bufs=10))
+
+        def step(i):
+            load(i + 4, narrow)
+            if len(staged) == len(loads):
+                flush()
+            quantize(i)
+
+        pending = []
+        step(4)
+        for q in range(4):
+            opened = [(d, q) for d in range(8)]
             for k in range(4):
-                multiply(d, q, k)
-            finish(d, q)
-
-        for i in range(LOADS_AHEAD):
-            load(i)
-        for i in range(4):
-            step(i)
-        first = [(d, 0) for d in range(OPEN_TILES)]
-        for k in range(4):
-            step(4 + k)
-            for d, q in first:
-                multiply(d, q, k)
-        for d, q in first[:2]:
-            finish(d, q)
-        step(8)
-        for d, q in first[2:]:
-            finish(d, q)
-        whole(8, 0)
-        whole(9, 0)
-        step(9)
-        for d in range(0, 4):
-            whole(d, 1)
-        step(10)
-        for d in range(4, 8):
-            whole(d, 1)
-        step(11)
-        for d in range(8, 10):
-            whole(d, 1)
-        second = [(d, q) for d in range(4) for q in (2, 3)]
-        for k in range(3):
-            for d, q in second:
-                multiply(d, q, k)
-        step(12)
-        for d, q in second:
-            multiply(d, q, 3)
-        for d, q in second:
-            finish(d, q)
-        for d in range(4, 10):
-            for q in (2, 3):
-                whole(d, q)
+                if k > 0:
+                    step(4 + 4 * q + k)
+                if k == 1:
+                    for d, qq in pending:
+                        finish(d, qq)
+                    for d, qq in opened:
+                        multiply(d, qq, 0)
+                if k > 0:
+                    for d, qq in opened:
+                        multiply(d, qq, k)
+            if q < 3:
+                step(4 + 4 * (q + 1))
+            for d, qq in opened:
+                finish(d, qq)
+            pending = [(8, q), (9, q)]
+            for d, qq in pending:
+                for k in range(4):
+                    multiply(d, qq, k)
+        for d, qq in pending:
+            finish(d, qq)

@@ -21,7 +21,7 @@ HALF = H // 2
 D_TILES = D // D_TILE
 
 
-EARLY = 4
+STORES = ((0, 5, 0, 2), (5, 5, 0, 2), (0, 8, 2, 1), (0, 4, 3, 1), (4, 4, 3, 1), (8, 2, 2, 2))
 
 
 def tile_mix_tied_none_kernel(tc, x, de, dr, e, out):
@@ -52,7 +52,8 @@ def tile_mix_tied_none_kernel(tc, x, de, dr, e, out):
             op, c, col, width = loads[i]
             raw = pool.tile([P, PACK, width], F32, name="raw", align_bytes=64)
             rows = sources[op][0][c * T_PASS : (c + 1) * T_PASS, col : col + width]
-            nc.sync.dma_start(out=raw[:], in_=rows.rearrange("(p j) w -> p j w", j=PACK))
+            queue = nc.sync if i % 2 == 0 else nc.scalar
+            queue.dma_start(out=raw[:], in_=rows.rearrange("(p j) w -> p j w", j=PACK))
             staged[i] = raw
 
         def quantize(i):
@@ -79,7 +80,7 @@ def tile_mix_tied_none_kernel(tc, x, de, dr, e, out):
                             in_=m[:, 0 : w * PACK],
                         )
 
-        acc, result = {}, {}
+        acc, result, left_in = {}, {}, {}
         count = [0]
         waiting = []
 
@@ -99,31 +100,34 @@ def tile_mix_tied_none_kernel(tc, x, de, dr, e, out):
                 stop=(k == 3),
             )
 
-        def store(d, lo, hi):
-            nc.sync.dma_start(out=out[d * D_TILE : (d + 1) * D_TILE, lo:hi], in_=result[d][:, lo:hi])
-
-        def finish(d, q):
-            if q == 0:
-                result[d] = outs.tile([P, H], F32, name="result", align_bytes=64)
-            cols = slice(q * H_TILE, (q + 1) * H_TILE)
-            if count[0] % 2 == 0:
-                nc.vector.tensor_copy(out=result[d][:, cols], in_=acc[d, q][:])
-            else:
-                nc.scalar.copy(out=result[d][:, cols], in_=acc[d, q][:])
-            count[0] += 1
-            if q == 1:
-                waiting.append((d, 0, HALF))
-            elif q == 2 and d < EARLY:
-                waiting.append((d, HALF, HALF + H_TILE))
-            elif q == 3:
-                waiting.append((d, HALF + (H_TILE if d < EARLY else 0), H))
-            if len(staged) == len(loads):
-                flush()
+        def store(group):
+            d0, ds, q0, qs = group
+            rows = out[d0 * D_TILE : (d0 + ds) * D_TILE, q0 * H_TILE : (q0 + qs) * H_TILE]
+            queue = nc.scalar if group == STORES[1] else nc.sync
+            queue.dma_start(out=rows.rearrange("(a p) h -> p a h", p=P), in_=result[group][:])
 
         def flush():
-            for d, lo, hi in waiting:
-                store(d, lo, hi)
+            for group in waiting:
+                store(group)
             waiting.clear()
+
+        def finish(d, q):
+            group = [s for s in STORES if s[0] <= d < s[0] + s[1] and s[2] <= q < s[2] + s[3]][0]
+            d0, ds, q0, qs = group
+            if group not in result:
+                result[group] = outs.tile([P, ds, qs * H_TILE], F32, name=f"result_{d0}_{q0}", align_bytes=64)
+                left_in[group] = ds * qs
+            target = result[group][:, d - d0, (q - q0) * H_TILE : (q - q0 + 1) * H_TILE]
+            if count[0] % 2 == 0:
+                nc.vector.tensor_copy(out=target, in_=acc[d, q][:])
+            else:
+                nc.scalar.copy(out=target, in_=acc[d, q][:])
+            count[0] += 1
+            left_in[group] -= 1
+            if left_in[group] == 0:
+                waiting.append(group)
+            if len(staged) == len(loads):
+                flush()
 
         with tc.tile_pool(name="whole", bufs=4) as whole:
             for i in range(4):
@@ -132,7 +136,7 @@ def tile_mix_tied_none_kernel(tc, x, de, dr, e, out):
                 load(i + 4, narrow)
                 quantize(i)
 
-        outs = ctx.enter_context(tc.tile_pool(name="outs", bufs=10))
+        outs = ctx.enter_context(tc.tile_pool(name="outs", bufs=1))
 
         def step(i):
             load(i + 4, narrow)

@@ -17,20 +17,29 @@ PACK = 4
 T_PASS = P * PACK
 D_TILE = 128
 H_TILE = 512
-HALF = H // 2
+HALF = 2 * H_TILE
 D_TILES = D // D_TILE
+BANKS = 8
+LOADS_AHEAD = 3
 
+PASSES = (("x", "de", 0), ("x", "de", 1), ("dr", "e", 0), ("dr", "e", 1))
 
-STORES = ((0, 5, 0, 2), (5, 5, 0, 2), (0, 8, 2, 1), (0, 4, 3, 1), (4, 4, 3, 1), (8, 2, 2, 2))
+PIECES = {
+    D: ((0, 512), (1024, 256), (512, 512)),
+    HALF: ((0, 512), (512, 512)),
+    H_TILE: ((0, 256), (256, 256)),
+}
+
+STORES = ((0, 5, 0, 2), (5, 5, 0, 2), (0, 2, 2, 2), (2, 2, 2, 2), (4, 1, 2, 2), (5, 1, 2, 2), (6, 1, 2, 2), (7, 1, 2, 2), (8, 1, 2, 2), (9, 1, 2, 1), (9, 1, 3, 1))
 
 
 def tile_mix_tied_none_kernel(tc, x, de, dr, e, out):
     nc = tc.nc
     with ExitStack() as ctx:
         keep = ctx.enter_context(tc.tile_pool(name="keep", bufs=1))
-        narrow = ctx.enter_context(tc.tile_pool(name="narrow", bufs=5))
+        moving = ctx.enter_context(tc.tile_pool(name="moving", bufs=LOADS_AHEAD + 1))
         mids = ctx.enter_context(tc.tile_pool(name="mids", bufs=2))
-        psum = ctx.enter_context(tc.psum_pool(name="psum", bufs=8))
+        psum = ctx.enter_context(tc.psum_pool(name="psum", bufs=BANKS))
         ctx.enter_context(tc.manual_schedule())
 
         codes, scales = {}, {}
@@ -41,9 +50,9 @@ def tile_mix_tied_none_kernel(tc, x, de, dr, e, out):
                 codes[op, c] = keep.tile([P, width], U32, name=f"codes_{op}{c}", align_bytes=64)
                 scales[op, c] = keep.tile([P, width], U8, name=f"scales_{op}{c}", align_bytes=64)
 
-        passes = (("x", "de", 0), ("x", "de", 1), ("dr", "e", 0), ("dr", "e", 1))
-        loads = [(left, c, 0, D) for left, rr, c in passes]
-        loads += [(right, c, q * H_TILE, H_TILE) for q in range(4) for ll, right, c in passes]
+        loads = [(left, c, 0, D) for left, right, c in PASSES]
+        for col, width in ((0, H_TILE), (H_TILE, H_TILE), (HALF, HALF)):
+            loads += [(right, c, col, width) for left, right, c in PASSES]
         staged = {}
 
         def load(i, pool):
@@ -58,114 +67,122 @@ def tile_mix_tied_none_kernel(tc, x, de, dr, e, out):
 
         def quantize(i):
             op, c, col, width = loads[i]
-            raw = staged[i]
-            pieces = [("v", 0, 512), ("s", 512, 512), ("v", 1024, 256)] if width == D else [("v", 0, 256), ("s", 256, 256)]
             ready = []
-            for eng, at, w in pieces:
-                m = mids.tile([P, H_TILE * PACK], BF16, name="mid_" + eng, align_bytes=64)
-                dst = m[:, 0 : w * PACK].rearrange("p (g i j) -> p g j i", i=4, j=PACK)
-                src = raw[:, :, at : at + w].rearrange("p j (g i) -> p g j i", i=4)
-                if eng == "v":
-                    nc.vector.tensor_copy(out=dst, in_=src)
-                else:
+            for n, (at, w) in enumerate(PIECES[width]):
+                by_scalar = n == len(PIECES[width]) - 1
+                mid = mids.tile([P, H_TILE * PACK], BF16, name="mid_s" if by_scalar else "mid_v", align_bytes=64)
+                dst = mid[:, 0 : w * PACK].rearrange("p (g i j) -> p g j i", i=4, j=PACK)
+                src = staged[i][:, :, at : at + w].rearrange("p j (g i) -> p g j i", i=4)
+                if by_scalar:
                     nc.scalar.copy(out=dst, in_=src)
-                ready.append((eng, m, at, w))
-            for want in ("v", "s"):
-                for eng, m, at, w in ready:
-                    if eng == want:
-                        cols = slice(col + at, col + at + w)
-                        nc.vector.quantize_mx(
-                            out=codes[op, c][:, cols].bitcast(sources[op][1]),
-                            scales=scales[op, c][:, cols],
-                            in_=m[:, 0 : w * PACK],
-                        )
+                else:
+                    nc.vector.tensor_copy(out=dst, in_=src)
+                ready.append((mid, at, w))
+            for mid, at, w in ready:
+                cols = slice(col + at, col + at + w)
+                nc.vector.quantize_mx(
+                    out=codes[op, c][:, cols].bitcast(sources[op][1]),
+                    scales=scales[op, c][:, cols],
+                    in_=mid[:, 0 : w * PACK],
+                )
 
-        acc, result, left_in = {}, {}, {}
-        count = [0]
-        waiting = []
+        acc, result, missing = {}, {}, {}
+        finished, complete = [], []
 
         def multiply(d, q, k):
-            left, right, c = passes[k]
+            left, right, c = PASSES[k]
             if k == 0:
                 acc[d, q] = psum.tile([P, H_TILE], F32, name="acc")
-            dc = slice(d * D_TILE, (d + 1) * D_TILE)
-            hc = slice(q * H_TILE, (q + 1) * H_TILE)
+            d_cols = slice(d * D_TILE, (d + 1) * D_TILE)
+            h_cols = slice(q * H_TILE, (q + 1) * H_TILE)
             nc.tensor.matmul_mx(
                 out=acc[d, q][:],
-                lhsT=codes[left, c][:, dc].bitcast(sources[left][1]),
-                lhsT_scale=scales[left, c][:, dc],
-                rhs=codes[right, c][:, hc].bitcast(sources[right][1]),
-                rhs_scale=scales[right, c][:, hc],
+                lhsT=codes[left, c][:, d_cols].bitcast(sources[left][1]),
+                lhsT_scale=scales[left, c][:, d_cols],
+                rhs=codes[right, c][:, h_cols].bitcast(sources[right][1]),
+                rhs_scale=scales[right, c][:, h_cols],
                 start=(k == 0),
-                stop=(k == 3),
+                stop=(k == len(PASSES) - 1),
             )
 
-        def store(group):
-            d0, ds, q0, qs = group
-            rows = out[d0 * D_TILE : (d0 + ds) * D_TILE, q0 * H_TILE : (q0 + qs) * H_TILE]
-            queue = nc.scalar if group == STORES[1] else nc.sync
-            queue.dma_start(out=rows.rearrange("(a p) h -> p a h", p=P), in_=result[group][:])
-
-        def flush():
-            for group in waiting:
-                store(group)
-            waiting.clear()
+        def store_complete():
+            if len(staged) < len(loads):
+                return
+            for group in complete:
+                d0, ds, q0, qs = group
+                rows = out[d0 * D_TILE : (d0 + ds) * D_TILE, q0 * H_TILE : (q0 + qs) * H_TILE]
+                nc.sync.dma_start(out=rows.rearrange("(a p) h -> p a h", p=P), in_=result[group][:])
+            complete.clear()
 
         def finish(d, q):
             group = [s for s in STORES if s[0] <= d < s[0] + s[1] and s[2] <= q < s[2] + s[3]][0]
             d0, ds, q0, qs = group
             if group not in result:
                 result[group] = outs.tile([P, ds, qs * H_TILE], F32, name=f"result_{d0}_{q0}", align_bytes=64)
-                left_in[group] = ds * qs
+                missing[group] = ds * qs
             target = result[group][:, d - d0, (q - q0) * H_TILE : (q - q0 + 1) * H_TILE]
-            if count[0] % 2 == 0:
+            if len(finished) % 2 == 0:
                 nc.vector.tensor_copy(out=target, in_=acc[d, q][:])
             else:
                 nc.scalar.copy(out=target, in_=acc[d, q][:])
-            count[0] += 1
-            left_in[group] -= 1
-            if left_in[group] == 0:
-                waiting.append(group)
-            if len(staged) == len(loads):
-                flush()
+            finished.append((d, q))
+            missing[group] -= 1
+            if missing[group] == 0:
+                complete.append(group)
+            store_complete()
 
-        with tc.tile_pool(name="whole", bufs=4) as whole:
-            for i in range(4):
-                load(i, whole)
-            for i in range(4):
-                load(i + 4, narrow)
-                quantize(i)
-
-        outs = ctx.enter_context(tc.tile_pool(name="outs", bufs=1))
+        def whole_sum(d, q):
+            for k in range(len(PASSES)):
+                multiply(d, q, k)
+            finish(d, q)
 
         def step(i):
-            load(i + 4, narrow)
-            if len(staged) == len(loads):
-                flush()
+            load(i + LOADS_AHEAD, moving)
+            store_complete()
             quantize(i)
 
-        pending = []
-        step(4)
-        for q in range(4):
-            opened = [(d, q) for d in range(8)]
-            for k in range(4):
-                if k > 0:
-                    step(4 + 4 * q + k)
-                if k == 1:
-                    for d, qq in pending:
-                        finish(d, qq)
-                    for d, qq in opened:
-                        multiply(d, qq, 0)
-                if k > 0:
-                    for d, qq in opened:
-                        multiply(d, qq, k)
-            if q < 3:
-                step(4 + 4 * (q + 1))
-            for d, qq in opened:
-                finish(d, qq)
-            pending = [(8, q), (9, q)]
-            for d, qq in pending:
-                for k in range(4):
-                    multiply(d, qq, k)
-        for d, qq in pending:
-            finish(d, qq)
+        with tc.tile_pool(name="stationary", bufs=len(PASSES)) as stationary:
+            for i in range(len(PASSES)):
+                load(i, stationary)
+            for i in range(len(PASSES)):
+                if i > 0:
+                    load(i + LOADS_AHEAD, moving)
+                quantize(i)
+        outs = ctx.enter_context(tc.tile_pool(name="outs", bufs=1))
+
+        opened = [(d, 0) for d in range(BANKS)]
+        for k in range(len(PASSES)):
+            step(4 + k)
+            for d, q in opened:
+                multiply(d, q, k)
+        for d, q in opened[:2]:
+            finish(d, q)
+        step(8)
+        for d, q in opened[2:]:
+            finish(d, q)
+        whole_sum(8, 0)
+        step(9)
+        whole_sum(9, 0)
+        step(10)
+        step(11)
+
+        step(12)
+        for d in range(5):
+            whole_sum(d, 1)
+        step(13)
+        for d in range(5, D_TILES):
+            whole_sum(d, 1)
+        step(14)
+
+        opened = [(d, q) for d in range(BANKS // 2) for q in (2, 3)]
+        for k in range(3):
+            for d, q in opened:
+                multiply(d, q, k)
+        step(15)
+        for d, q in opened:
+            multiply(d, q, 3)
+        for d, q in opened:
+            finish(d, q)
+        for d in range(BANKS // 2, D_TILES):
+            for q in (2, 3):
+                whole_sum(d, q)

@@ -37,7 +37,8 @@ def tile_mix_tied_none_kernel(tc, x, de, dr, e, out):
     nc = tc.nc
     with ExitStack() as ctx:
         keep = ctx.enter_context(tc.tile_pool(name="keep", bufs=1))
-        moving = ctx.enter_context(tc.tile_pool(name="moving", bufs=LOADS_AHEAD + 1))
+        halves = ctx.enter_context(tc.tile_pool(name="halves", bufs=3))
+        quarters = ctx.enter_context(tc.tile_pool(name="quarters", bufs=3))
         mids = ctx.enter_context(tc.tile_pool(name="mids", bufs=2))
         psum = ctx.enter_context(tc.psum_pool(name="psum", bufs=BANKS))
         ctx.enter_context(tc.manual_schedule())
@@ -51,18 +52,20 @@ def tile_mix_tied_none_kernel(tc, x, de, dr, e, out):
                 scales[op, c] = keep.tile([P, width], U8, name=f"scales_{op}{c}", align_bytes=64)
 
         loads = [(left, c, 0, D) for left, right, c in PASSES]
-        for col, width in ((0, H_TILE), (H_TILE, H_TILE), (HALF, HALF)):
-            loads += [(right, c, col, width) for left, right, c in PASSES]
+        loads += [("de", 0, 0, HALF), ("de", 1, 0, HALF)]
+        loads += [("e", c, q * H_TILE, H_TILE) for q in (0, 1) for c in (0, 1)]
+        loads += [("de", 0, HALF, HALF), ("de", 1, HALF, HALF), ("e", 0, HALF, HALF)]
+        loads += [("e", 1, q * H_TILE, H_TILE) for q in (2, 3)]
         staged = {}
 
-        def load(i, pool):
+        def load(i):
             if i >= len(loads):
                 return
             op, c, col, width = loads[i]
+            pool = stationary if width == D else halves if width == HALF else quarters
             raw = pool.tile([P, PACK, width], F32, name="raw", align_bytes=64)
             rows = sources[op][0][c * T_PASS : (c + 1) * T_PASS, col : col + width]
-            queue = nc.sync if i % 2 == 0 else nc.scalar
-            queue.dma_start(out=raw[:], in_=rows.rearrange("(p j) w -> p j w", j=PACK))
+            nc.sync.dma_start(out=raw[:], in_=rows.rearrange("(p j) w -> p j w", j=PACK))
             staged[i] = raw
 
         def quantize(i):
@@ -137,17 +140,15 @@ def tile_mix_tied_none_kernel(tc, x, de, dr, e, out):
             finish(d, q)
 
         def step(i):
-            load(i + LOADS_AHEAD, moving)
-            store_complete()
             quantize(i)
+            load(i + LOADS_AHEAD)
+            store_complete()
 
-        with tc.tile_pool(name="stationary", bufs=len(PASSES)) as stationary:
+        with tc.tile_pool(name="stationary", bufs=3) as stationary:
+            for i in range(LOADS_AHEAD):
+                load(i)
             for i in range(len(PASSES)):
-                load(i, stationary)
-            for i in range(len(PASSES)):
-                if i > 0:
-                    load(i + LOADS_AHEAD, moving)
-                quantize(i)
+                step(i)
         outs = ctx.enter_context(tc.tile_pool(name="outs", bufs=1))
 
         opened = [(d, 0) for d in range(BANKS)]
@@ -163,24 +164,24 @@ def tile_mix_tied_none_kernel(tc, x, de, dr, e, out):
         whole_sum(8, 0)
         step(9)
         whole_sum(9, 0)
-        step(10)
-        step(11)
 
-        step(12)
+        step(10)
         for d in range(5):
             whole_sum(d, 1)
-        step(13)
+        step(11)
         for d in range(5, D_TILES):
             whole_sum(d, 1)
-        step(14)
+        step(12)
 
         opened = [(d, q) for d in range(BANKS // 2) for q in (2, 3)]
         for k in range(3):
             for d, q in opened:
                 multiply(d, q, k)
-        step(15)
-        for d, q in opened:
-            multiply(d, q, 3)
+        for h_tile in (2, 3):
+            step(11 + h_tile)
+            for d, q in opened:
+                if q == h_tile:
+                    multiply(d, q, 3)
         for d, q in opened:
             finish(d, q)
         for d in range(BANKS // 2, D_TILES):

from contextlib import ExitStack

import concourse.mybir as mybir

T, D, H = 1024, 1280, 2048
FLOPS = 2 * (2 * T * D * H)

F32 = mybir.dt.float32
BF16 = mybir.dt.bfloat16
U32 = mybir.dt.uint32
U8 = mybir.dt.uint8
E4M3 = mybir.dt.float8_e4m3fn_x4
E5M2 = mybir.dt.float8_e5m2_x4

P = 128
PACK = 4
T_PASS = P * PACK
D_TILE = 128
H_TILE = 512
HALF = 2 * H_TILE
D_TILES = D // D_TILE
BANKS = 8
LOADS_AHEAD = 3

PASSES = (("x", "de", 0), ("x", "de", 1), ("dr", "e", 0), ("dr", "e", 1))

PIECES = {
    D: ((0, 512), (1024, 256), (512, 512)),
    HALF: ((0, 512), (512, 512)),
    H_TILE: ((0, 256), (256, 256)),
}

STORES = ((0, 5, 0, 2), (5, 5, 0, 2), (0, 2, 2, 2), (2, 2, 2, 2), (4, 1, 2, 2), (5, 1, 2, 2), (6, 1, 2, 2), (7, 1, 2, 2), (8, 1, 2, 2), (9, 1, 2, 1), (9, 1, 3, 1))


def tile_mix_tied_none_kernel(tc, x, de, dr, e, out):
    nc = tc.nc
    with ExitStack() as ctx:
        keep = ctx.enter_context(tc.tile_pool(name="keep", bufs=1))
        halves = ctx.enter_context(tc.tile_pool(name="halves", bufs=3))
        quarters = ctx.enter_context(tc.tile_pool(name="quarters", bufs=3))
        mids = ctx.enter_context(tc.tile_pool(name="mids", bufs=2))
        psum = ctx.enter_context(tc.psum_pool(name="psum", bufs=BANKS))
        ctx.enter_context(tc.manual_schedule())

        codes, scales = {}, {}
        sources = {"x": (x, E4M3), "de": (de, E5M2), "dr": (dr, E5M2), "e": (e, E4M3)}
        for op in sources:
            width = sources[op][0].shape[1]
            for c in range(T // T_PASS):
                codes[op, c] = keep.tile([P, width], U32, name=f"codes_{op}{c}", align_bytes=64)
                scales[op, c] = keep.tile([P, width], U8, name=f"scales_{op}{c}", align_bytes=64)

        loads = [(left, c, 0, D) for left, right, c in PASSES]
        loads += [("de", 0, 0, HALF), ("de", 1, 0, HALF)]
        loads += [("e", c, q * H_TILE, H_TILE) for q in (0, 1) for c in (0, 1)]
        loads += [("de", 0, HALF, HALF), ("de", 1, HALF, HALF), ("e", 0, HALF, HALF)]
        loads += [("e", 1, q * H_TILE, H_TILE) for q in (2, 3)]
        staged = {}

        def load(i):
            if i >= len(loads):
                return
            op, c, col, width = loads[i]
            pool = stationary if width == D else halves if width == HALF else quarters
            raw = pool.tile([P, PACK, width], F32, name="raw", align_bytes=64)
            rows = sources[op][0][c * T_PASS : (c + 1) * T_PASS, col : col + width]
            nc.sync.dma_start(out=raw[:], in_=rows.rearrange("(p j) w -> p j w", j=PACK))
            staged[i] = raw

        def quantize(i):
            op, c, col, width = loads[i]
            ready = []
            for n, (at, w) in enumerate(PIECES[width]):
                by_scalar = n == len(PIECES[width]) - 1
                mid = mids.tile([P, H_TILE * PACK], BF16, name="mid_s" if by_scalar else "mid_v", align_bytes=64)
                dst = mid[:, 0 : w * PACK].rearrange("p (g i j) -> p g j i", i=4, j=PACK)
                src = staged[i][:, :, at : at + w].rearrange("p j (g i) -> p g j i", i=4)
                if by_scalar:
                    nc.scalar.copy(out=dst, in_=src)
                else:
                    nc.vector.tensor_copy(out=dst, in_=src)
                ready.append((mid, at, w))
            for mid, at, w in ready:
                cols = slice(col + at, col + at + w)
                nc.vector.quantize_mx(
                    out=codes[op, c][:, cols].bitcast(sources[op][1]),
                    scales=scales[op, c][:, cols],
                    in_=mid[:, 0 : w * PACK],
                )

        acc, result, missing = {}, {}, {}
        finished, complete = [], []

        def multiply(d, q, k):
            left, right, c = PASSES[k]
            if k == 0:
                acc[d, q] = psum.tile([P, H_TILE], F32, name="acc")
            d_cols = slice(d * D_TILE, (d + 1) * D_TILE)
            h_cols = slice(q * H_TILE, (q + 1) * H_TILE)
            nc.tensor.matmul_mx(
                out=acc[d, q][:],
                lhsT=codes[left, c][:, d_cols].bitcast(sources[left][1]),
                lhsT_scale=scales[left, c][:, d_cols],
                rhs=codes[right, c][:, h_cols].bitcast(sources[right][1]),
                rhs_scale=scales[right, c][:, h_cols],
                start=(k == 0),
                stop=(k == len(PASSES) - 1),
            )

        def store_complete():
            if len(staged) < len(loads):
                return
            for group in complete:
                d0, ds, q0, qs = group
                rows = out[d0 * D_TILE : (d0 + ds) * D_TILE, q0 * H_TILE : (q0 + qs) * H_TILE]
                nc.sync.dma_start(out=rows.rearrange("(a p) h -> p a h", p=P), in_=result[group][:])
            complete.clear()

        def finish(d, q):
            group = [s for s in STORES if s[0] <= d < s[0] + s[1] and s[2] <= q < s[2] + s[3]][0]
            d0, ds, q0, qs = group
            if group not in result:
                result[group] = outs.tile([P, ds, qs * H_TILE], F32, name=f"result_{d0}_{q0}", align_bytes=64)
                missing[group] = ds * qs
            target = result[group][:, d - d0, (q - q0) * H_TILE : (q - q0 + 1) * H_TILE]
            if len(finished) % 2 == 0:
                nc.vector.tensor_copy(out=target, in_=acc[d, q][:])
            else:
                nc.scalar.copy(out=target, in_=acc[d, q][:])
            finished.append((d, q))
            missing[group] -= 1
            if missing[group] == 0:
                complete.append(group)
            store_complete()

        def whole_sum(d, q):
            for k in range(len(PASSES)):
                multiply(d, q, k)
            finish(d, q)

        def step(i):
            quantize(i)
            load(i + LOADS_AHEAD)
            store_complete()

        with tc.tile_pool(name="stationary", bufs=3) as stationary:
            for i in range(LOADS_AHEAD):
                load(i)
            for i in range(len(PASSES)):
                step(i)
        outs = ctx.enter_context(tc.tile_pool(name="outs", bufs=1))

        opened = [(d, 0) for d in range(BANKS)]
        for k in range(len(PASSES)):
            step(4 + k)
            for d, q in opened:
                multiply(d, q, k)
        for d, q in opened[:2]:
            finish(d, q)
        step(8)
        for d, q in opened[2:]:
            finish(d, q)
        whole_sum(8, 0)
        step(9)
        whole_sum(9, 0)

        step(10)
        for d in range(5):
            whole_sum(d, 1)
        step(11)
        for d in range(5, D_TILES):
            whole_sum(d, 1)
        step(12)

        opened = [(d, q) for d in range(BANKS // 2) for q in (2, 3)]
        for k in range(3):
            for d, q in opened:
                multiply(d, q, k)
        for h_tile in (2, 3):
            step(11 + h_tile)
            for d, q in opened:
                if q == h_tile:
                    multiply(d, q, 3)
        for d, q in opened:
            finish(d, q)
        for d in range(BANKS // 2, D_TILES):
            for q in (2, 3):
                whole_sum(d, q)
